import numpy as np
import ml_dtypes


def mxq(x, axis, fmt="e4m3"):
    dtype, down = {"e4m3": (ml_dtypes.float8_e4m3fn, 7), "e5m2": (ml_dtypes.float8_e5m2, 14)}[fmt]
    v = np.moveaxis(np.asarray(x, np.float32).astype(ml_dtypes.bfloat16).astype(np.float64), axis, -1)
    blocks = v.reshape(v.shape[:-1] + (-1, 32))
    amax = np.abs(blocks).max(-1, keepdims=True)
    byte = np.maximum(np.where(amax > 0, np.frexp(amax)[1] - 1 + 127, 0) - down, 1)
    scale = np.exp2(byte - 127.0)
    codes = (blocks / scale).astype(np.float32).astype(dtype).astype(np.float64)
    return np.moveaxis((codes * scale).reshape(v.shape), -1, axis)


WIDE = False


def mx_kscale(k):
    if not WIDE:
        return np.ones(k)
    levels = np.array([10, -10, 5, -5, 0])
    if k % 512:
        return np.exp2(np.random.permutation(np.resize(levels, k // 32))).repeat(32)
    a = np.empty((k // 512, 16))
    for p in range(k // 512):
        a[p, :8] = np.random.permutation(np.resize(levels, 8))
        for g in range(8):
            far = levels[np.abs(levels - a[p, g]) >= 10]
            a[p, g + 8] = far[np.random.randint(len(far))]
    return np.exp2(a.ravel()).repeat(32)


def f64(x):
    return np.asarray(x).astype(np.float64)


def striped(idx):
    return np.tile(idx.reshape(-1, 16).T, (8, 1)).astype(np.uint16)


def unstriped(offs):
    return offs[:16].T.reshape(-1).astype(np.int64)


E2M1 = np.array([0.0, 0.5, 1.0, 1.5, 2.0, 3.0, 4.0, 6.0, -0.0, -0.5, -1.0, -1.5, -2.0, -3.0, -4.0, -6.0])


def pack_weight(w, fmt):
    k, n = w.shape
    w = f64(np.asarray(w, np.float32).astype(ml_dtypes.bfloat16)).reshape(k // 32, 32, n)
    amax = np.abs(w).max(1)
    if fmt == "e4m3":
        byte = np.frexp(amax)[1] - 1 + 127 - 7
    else:
        mant, ex = np.frexp(amax / 6.0)
        byte = np.where(mant > 0.5, ex, ex - 1) + 127
    byte = np.clip(np.where(amax > 0, byte, 1), 1, 254)
    scaled = (w * np.exp2(127.0 - byte)[:, None, :]).reshape(k, n).astype(np.float32)
    by_word = np.ascontiguousarray(scaled.reshape(k // 512, 128, 4, n).transpose(0, 1, 3, 2))
    if fmt == "e4m3":
        words = by_word.astype(ml_dtypes.float8_e4m3fn).view(np.uint8)
    else:
        c = by_word.astype(ml_dtypes.float4_e2m1fn).view(np.uint8) & 0xF
        words = (c[..., 0::2] | (c[..., 1::2] << 4)).reshape(k // 512, 128, 2 * n)
    return np.ascontiguousarray(words), np.ascontiguousarray(byte.astype(np.uint8).reshape(k // 512, 16, n))


def unpack_weight(words, scales, fmt):
    g, _, n = scales.shape
    words = np.ascontiguousarray(words).reshape(g, 128, n, -1)
    if fmt == "e4m3":
        vals = words.view(ml_dtypes.float8_e4m3fn).astype(np.float64)
    else:
        nib = np.empty((g, 128, n, 4), np.uint8)
        nib[..., 0::2] = words & 0xF
        nib[..., 1::2] = words >> 4
        vals = E2M1[nib]
    vals = vals * np.repeat(np.exp2(scales.astype(np.float64) - 127.0), 8, axis=1)[..., None]
    return vals.transpose(0, 1, 3, 2).reshape(g * 512, n)


def gelu(v):
    return 0.5 * v * (1.0 + np.tanh(np.sqrt(2.0 / np.pi) * (v + 0.044715 * v**3)))


def often(T, S):
    return np.random.permutation(T)[(T * np.random.uniform(0, 1, S) ** 4).astype(np.int64)]


def bf(x):
    return np.asarray(x, np.float32).astype(ml_dtypes.bfloat16)


def planes(Y):
    n, m = Y.shape
    b = f64(bf(Y)).reshape(n // 32, 32, m)
    amax = np.abs(b).max(1)
    byte = np.clip(np.where(amax > 0, np.frexp(amax)[1] - 1 + 127 - 7, 1), 1, 254)
    codes = (b * np.exp2(127.0 - byte)[:, None, :]).reshape(n, m).astype(np.float32).astype(ml_dtypes.float8_e4m3fn).view(np.uint8)
    words = codes.reshape(n // 512, 128, 4, m).transpose(0, 1, 3, 2)
    return np.ascontiguousarray(words), np.ascontiguousarray(byte.astype(np.uint8).reshape(n // 512, 16, m))


K, K2, H, N, T, S, P = 1024, 512, 1024, 512, 2048, 1024, 512

def setup_inputs():
    n = np.random.standard_normal
    s, s2 = mx_kscale(K)[:, None], mx_kscale(K2)[:, None]
    u = mx_kscale(H)[:, None]
    size = np.exp(0.8 * n(N))
    d = {}
    d["tab_words"], d["tab_scales"] = pack_weight(n((K, T)) * s, "e4m3")
    d["tab2_words"], d["tab2_scales"] = pack_weight(n((K2, T)) * s2, "e4m3")
    d["tab3_words"], d["tab3_scales"] = pack_weight(n((K, T)) * s, "e4m3")
    d["offs"] = striped(np.random.permutation(T)[:S])
    d["offs2"] = striped(np.random.permutation(T)[:S])
    d["offs3"] = striped(np.random.permutation(T)[:S])
    d["pos1"] = striped(np.random.permutation(S)[:P])
    d["pos2"] = striped(often(S, P))
    d["pos3"] = striped(often(S, P))
    d["w1"] = (n((K, H)) / s / K**0.5).astype(np.float32)
    d["w2_words"], d["w2_scales"] = pack_weight(n((K2, H)) / s2 / K2**0.5, "e2m1")
    d["w3_words"], d["w3_scales"] = pack_weight(n((K, H)) / s / K**0.5, "e4m3")
    d["gain"] = (np.exp(0.3 * n(H)) * u[:, 0]).astype(np.float32)
    d["w4"] = (1.2 * n((H, N)) / u / H**0.5 * size[None, :]).astype(np.float32)
    d["base"] = (0.5 * n((N, P)) * size[:, None]).astype(np.float32)
    return d

def reference(tab_words, tab_scales, tab2_words, tab2_scales, tab3_words, tab3_scales, offs, offs2, offs3, pos1, pos2, pos3, w1, w2_words, w2_scales, w3_words, w3_scales, gain, w4, base):
    v = unpack_weight(tab_words, tab_scales, "e4m3")[:, unstriped(offs)]
    v2 = unpack_weight(tab2_words, tab2_scales, "e4m3")[:, unstriped(offs2)]
    v3 = unpack_weight(tab3_words, tab3_scales, "e4m3")[:, unstriped(offs3)]
    a = mxq(f64(w1), 0, "e4m3").T @ v
    b = unpack_weight(w2_words, w2_scales, "e2m1").T @ v2
    d = unpack_weight(w3_words, w3_scales, "e4m3").T @ v3
    a1 = a[:, unstriped(pos1)]
    lit = np.tanh(a1 + b[:, unstriped(pos2)])
    dev = np.tanh(a1 - d[:, unstriped(pos3)])
    z = lit * dev * f64(gain)[:, None]
    y = (mxq(f64(w4), 0, "e4m3").T @ mxq(z, 0, "e4m3")) + f64(base)
    words, scales = planes(y)
    return y, words, scales

@@ -1,0 +1,350 @@
+from contextlib import ExitStack
+
+import concourse.mybir as mybir
+from concourse.masks import make_identity
+
+K, K2, H, N, T, S, J = 1024, 512, 1024, 512, 2048, 1024, 512
+FLOPS = 2 * (K + K2 + K) * H * S + 2 * H * N * J
+
+F32 = mybir.dt.float32
+BF16 = mybir.dt.bfloat16
+I32 = mybir.dt.int32
+U32 = mybir.dt.uint32
+U16 = mybir.dt.uint16
+U8 = mybir.dt.uint8
+FP8X4 = mybir.dt.float8_e4m3fn_x4
+FP4X4 = mybir.dt.float4_e2m1fn_x4
+MULT = mybir.AluOpType.mult
+ADD = mybir.AluOpType.add
+SUBTRACT = mybir.AluOpType.subtract
+TANH = mybir.ActivationFunctionType.Tanh
+
+P = 128
+PASS = 512
+BANK = 512
+HALF = J // 2
+
+
+def tile_list_diamond_report_features_kernel(
+    tc, tab_words, tab_scales, tab2_words, tab2_scales, tab3_words, tab3_scales,
+    offs, offs2, offs3, pos1, pos2, pos3, w1, w2_words, w2_scales, w3_words, w3_scales,
+    gain, w4, base, out_0, out_1, out_2,
+):
+    nc = tc.nc
+    with ExitStack() as ctx:
+        held = ctx.enter_context(tc.tile_pool(name="held", bufs=1))
+        stage = ctx.enter_context(tc.tile_pool(name="stage", bufs=5))
+        rounded = ctx.enter_context(tc.tile_pool(name="rounded", bufs=3))
+        rows = ctx.enter_context(tc.tile_pool(name="rows", bufs=4))
+        picked = ctx.enter_context(tc.tile_pool(name="picked", bufs=3))
+        first_psum = ctx.enter_context(tc.psum_pool(name="first_psum", bufs=4))
+        last_psum = ctx.enter_context(tc.psum_pool(name="last_psum", bufs=4))
+
+        def keep(name, shape, dtype):
+            return held.tile(shape, dtype, name=name, align_bytes=64)
+
+        def load_list(name, src):
+            tile = held.tile(list(src.shape), U16, name=name)
+            nc.sync.dma_start(tile[:], src)
+            return tile
+
+        def zeroed_plane(name, width):
+            plane = keep(name, [P, width], U8)
+            nc.vector.memset(plane[:].bitcast(I32), 0)
+            return plane
+
+        def load_scales(queue, plane, src):
+            passes = src.shape[0]
+            for q in range(4):
+                queue.dma_start(
+                    plane[32 * q : 32 * q + 4 * passes, :].bitcast(I32),
+                    src[:, 4 * q : 4 * q + 4, :].bitcast(I32),
+                )
+
+        def load_words(src, kp):
+            tile = stage.tile([P, T], I32, name="staged", align_bytes=64)
+            nc.sync.dma_start(tile[:], src[kp].rearrange("p n i -> p (n i)").bitcast(I32))
+            return tile
+
+        def gather_words(name, window, idx):
+            out = keep(name, [P, S], U32)
+            nc.vector.tensor_copy(out[:], window[:].bitcast(U32).indirect(idx[:]))
+            return out
+
+        def gather_scales(name, window, idx):
+            out = keep(name, [P, S], U8)
+            nc.vector.tensor_copy(out[:], window[:].indirect(idx[:]))
+            return out
+
+        def deal(name, src, dtype):
+            out = keep(name, list(src.shape), dtype)
+            words = src[:].bitcast(I32)
+            nc.vector.tensor_copy(
+                out[:].bitcast(I32).rearrange("p (a t g w) -> p a t g w", a=2, t=4, g=16),
+                words.rearrange("p (a g t w) -> p a t g w", a=2, t=4, g=16),
+            )
+            return out
+
+        def load_w1(kp, a):
+            tile = stage.tile([P, 4, PASS], F32, name="staged", align_bytes=64)
+            src = w1[PASS * kp : PASS * (kp + 1), PASS * a : PASS * (a + 1)]
+            nc.sync.dma_start(tile[:], src.rearrange("(p j) c -> p j c", j=4))
+            return tile
+
+        def round_w1(raw):
+            out = rounded.tile([P, 4 * PASS], BF16, name="rounded", align_bytes=64)
+            nc.scalar.copy(
+                out[:].rearrange("p (t g i j) -> p t g i j", t=4, g=16, i=8),
+                raw[:].rearrange("p j (g t i) -> p t g i j", t=4, g=16),
+            )
+            return out
+
+        def load_w3(a):
+            tile = keep("w3_raw%d" % a, [P, 2 * PASS], I32)
+            src = w3_words[:, :, PASS * a : PASS * (a + 1), :].rearrange("k p n i -> p k (n i)")
+            nc.sync.dma_start(tile[:].rearrange("p (k n) -> p k n", k=2), src.bitcast(I32))
+            return tile
+
+        def load_w4(a):
+            tile = stage.tile([P, 4, N], F32, name="staged", align_bytes=64)
+            src = w4[PASS * a : PASS * (a + 1), :].rearrange("(g t i) n -> t g i n", t=4, i=8)
+            for t in range(4):
+                nc.sync.dma_start(tile[:, t, :], src[t])
+            return tile
+
+        def round_w4(raw):
+            out = rounded.tile([P, 4 * N], BF16, name="rounded", align_bytes=64)
+            nc.scalar.copy(
+                out[:].rearrange("p (u m t) -> p m u t", u=4, t=4),
+                raw[:].rearrange("p t (m u) -> p m u t", u=4),
+            )
+            return out
+
+        def quantize(name, values):
+            width = values.shape[1] // 4
+            codes = keep(name + "_codes", [P, width], U32)
+            scales = keep(name + "_scales", [P, width], U8)
+            nc.vector.quantize_mx(out=codes[:].bitcast(FP8X4), scales=scales[:], in_=values[:])
+            return codes, scales
+
+        def product_rows(tile, passes):
+            for c in range(S // BANK):
+                cols = slice(BANK * c, BANK * (c + 1))
+                bank = first_psum.tile([P, BANK], F32, name="bank")
+                for n, (lhs, lhs_scale, rhs, rhs_scale) in enumerate(passes):
+                    nc.tensor.matmul_mx(
+                        out=bank[:], lhsT=lhs, lhsT_scale=lhs_scale,
+                        rhs=rhs[:, cols].bitcast(FP8X4), rhs_scale=rhs_scale[:, cols],
+                        start=(n == 0), stop=(n == len(passes) - 1),
+                    )
+                nc.scalar.copy(tile[:, cols], bank[:])
+            return tile
+
+        v2_plane = zeroed_plane("v2_plane", T)
+        w2_plane = zeroed_plane("w2_plane", H)
+        v_plane = zeroed_plane("v_plane", T)
+        v3_plane = zeroed_plane("v3_plane", T)
+        w3_plane = zeroed_plane("w3_plane", H)
+
+        idx2 = load_list("idx2", offs2)
+        v2_raw = load_words(tab2_words, 0)
+        load_scales(nc.sync, v2_plane, tab2_scales)
+        w1_raw = {(0, 0): load_w1(0, 0)}
+        w2_raw = keep("w2_raw", [P, 2 * H], U8)
+        nc.sync.dma_start(w2_raw[:].bitcast(I32), w2_words[0].bitcast(I32))
+        load_scales(nc.sync, w2_plane, w2_scales)
+        v_raw = [load_words(tab_words, 0)]
+        idx = load_list("idx", offs)
+        v_raw.append(load_words(tab_words, 1))
+        load_scales(nc.sync, v_plane, tab_scales)
+        w1_raw[1, 0] = load_w1(1, 0)
+        idx3 = load_list("idx3", offs3)
+
+        v2 = gather_words("v2", v2_raw, idx2)
+        v2_scale = gather_scales("v2_scale", v2_plane, idx2)
+        w2_scale = deal("w2_scale", w2_plane, U8)
+        w2 = deal("w2", w2_raw, U8)
+
+        v3_raw = [load_words(tab3_words, 0)]
+        load_scales(nc.sync, v3_plane, tab3_scales)
+        v = [gather_words("v_%d" % kp, v_raw[kp], idx) for kp in range(2)]
+        v3_raw.append(load_words(tab3_words, 1))
+        load_scales(nc.sync, w3_plane, w3_scales)
+        w3_raw = [load_w3(0)]
+        p1 = load_list("p1", pos1)
+        p2 = load_list("p2", pos2)
+        p3 = load_list("p3", pos3)
+        v_scale = gather_scales("v_scale", v_plane, idx)
+
+        w1_q = {}
+        for kp in range(2):
+            w1_q[kp, 0] = quantize("w1_%d0" % kp, round_w1(w1_raw[kp, 0]))
+            w1_raw[kp, 1] = load_w1(kp, 1)
+        w3_raw.append(load_w3(1))
+
+        def b_rows(s):
+            tile = keep("b%d" % s, [P, S], F32)
+            return product_rows(tile, [(
+                w2[:, 2 * P * s : 2 * P * (s + 1)].bitcast(FP4X4), w2_scale[:, P * s : P * (s + 1)],
+                v2, v2_scale,
+            )])
+
+        def a_rows(s):
+            a, t = divmod(s, 4)
+            cols = slice(P * t, P * (t + 1))
+            tile = rows.tile([P, S], F32, name="a_rows")
+            return product_rows(tile, [
+                (w1_q[kp, a][0][:, cols].bitcast(FP8X4), w1_q[kp, a][1][:, cols], v[kp], v_scale[4 * kp : P, :])
+                for kp in range(2)
+            ])
+
+        def d_rows(s):
+            a, t = divmod(s, 4)
+            tile = rows.tile([P, S], F32, name="d_rows")
+            return product_rows(tile, [
+                (
+                    w3[a][:, PASS * kp + P * t : PASS * kp + P * (t + 1)].bitcast(FP8X4),
+                    w3_scale[4 * kp : P, P * s : P * (s + 1)], v3[kp], v3_scale[4 * kp : P, :],
+                )
+                for kp in range(2)
+            ])
+
+        b_win = [b_rows(s) for s in range(8)]
+
+        identity = keep("identity", [P, P], F32)
+        make_identity(nc, identity[:])
+        gain_rows = keep("gain_rows", [P, P], F32)
+        nc.gpsimd.memset(gain_rows[:], 0.0)
+        for a in range(2):
+            nc.gpsimd.dma_start(
+                gain_rows[4 * a : 4 * a + 4, :].rearrange("t (g i) -> t g i", i=8),
+                gain[PASS * a : PASS * (a + 1)].rearrange("(g t i) -> t g i", t=4, i=8),
+            )
+        gain_bank = first_psum.tile([P, P], F32, name="bank")
+        nc.tensor.transpose(gain_bank[:], gain_rows[:], identity[:])
+        gain_cols = keep("gain_cols", [P, 8], F32)
+        nc.scalar.copy(gain_cols[:], gain_bank[:, 0:8])
+
+        v3 = [gather_words("v3_%d" % kp, v3_raw[kp], idx3) for kp in range(2)]
+        v3_scale = gather_scales("v3_scale", v3_plane, idx3)
+        w3_scale = deal("w3_scale", w3_plane, U8)
+        w3 = [deal("w3_0", w3_raw[0], U32)]
+
+        w4_raw = [load_w4(a) for a in range(2)]
+        base_sb = keep("base_sb", [P, 4, J], F32)
+        nc.sync.dma_start(base_sb[:], base.rearrange("(p u) j -> p u j", u=4))
+
+        a_win = {s: a_rows(s) for s in range(4)}
+        w1_round = round_w1(w1_raw[0, 1])
+        d_win = {s: d_rows(s) for s in range(2)}
+
+        steps = [(s, 0, J) for s in range(4)]
+        steps = steps + [(s, HALF * h, HALF) for h in range(2) for s in range(4, 8)]
+        z_planes = {}
+        a1, lit, dev = {}, {}, {}
+
+        def pick_a(n):
+            s, j0, width = steps[n]
+            a1[n] = picked.tile([P, width], F32, name="a1", bufs=2)
+            nc.vector.tensor_copy(a1[n][:], a_win[s][:].indirect(p1[:, j0 // 16 : (j0 + width) // 16]))
+
+        def join(n):
+            s, j0, width = steps[n]
+            cols = slice(j0 // 16, (j0 + width) // 16)
+            lit[n] = picked.tile([P, width], F32, name="lit")
+            nc.vector.tensor_tensor(lit[n][:], b_win[s][:].indirect(p2[:, cols]), a1[n][:], ADD)
+            nc.scalar.activation(lit[n][:], lit[n][:], TANH)
+            dev[n] = picked.tile([P, width], F32, name="dev")
+            nc.vector.tensor_tensor(dev[n][:], d_win[s][:].indirect(p3[:, cols]), a1[n][:], SUBTRACT)
+            nc.scalar.activation(dev[n][:], dev[n][:], TANH, scale=-1.0)
+
+        def multiply(n):
+            s, j0, width = steps[n]
+            group = n // 4
+            if group not in z_planes:
+                z_planes[group] = keep("z_planes%d" % group, [P, 4, width], BF16)
+            nc.vector.scalar_tensor_tensor(
+                z_planes[group][:, s % 4, :], lit[n][:], gain_cols[:, s : s + 1], dev[n][:], MULT, MULT
+            )
+
+        def weave(engine_copy, planes):
+            width = planes.shape[2]
+            out = rounded.tile([P, 4 * width], BF16, name="rounded", align_bytes=64)
+            engine_copy(out[:].rearrange("p (j t) -> p j t", t=4), planes[:].rearrange("p t j -> p j t"))
+            return out
+
+        y_codes = keep("y_codes", [P, J], U32)
+        y_scales = keep("y_scales", [P, J], U8)
+        w4_q, z_q, y_banks, y_half = {}, {}, {}, {}
+
+        def last_pass(h, a):
+            codes, scales = z_q[a * (1 + h)]
+            j0 = HALF * h * (1 - a)
+            for u in range(4):
+                if a == 0:
+                    y_banks[h, u] = last_psum.tile([P, HALF], F32, name="y_bank")
+                nc.tensor.matmul_mx(
+                    out=y_banks[h, u][:],
+                    lhsT=w4_q[a][0][:, P * u : P * (u + 1)].bitcast(FP8X4),
+                    lhsT_scale=w4_q[a][1][:, P * u : P * (u + 1)],
+                    rhs=codes[:, j0 : j0 + HALF].bitcast(FP8X4), rhs_scale=scales[:, j0 : j0 + HALF],
+                    start=(a == 0), stop=(a == 1),
+                )
+
+        def add_base(h):
+            cols = slice(HALF * h, HALF * (h + 1))
+            y_half[h] = keep("y%d" % h, [P, 4, HALF], F32)
+            for u in range(4):
+                nc.vector.tensor_tensor(y_half[h][:, u, :], y_banks[h, u][:], base_sb[:, u, cols], ADD)
+            nc.sync.dma_start(out_0.rearrange("(p u) j -> p u j", u=4)[:, :, cols], y_half[h][:])
+
+        def y_planes(h, woven):
+            cols = slice(HALF * h, HALF * (h + 1))
+            nc.vector.quantize_mx(out=y_codes[:, cols].bitcast(FP8X4), scales=y_scales[:, cols], in_=woven[:])
+            nc.scalar.dma_start(
+                out_1[0].rearrange("p m t -> p (m t)").bitcast(I32)[:, cols], y_codes[:, cols].bitcast(I32)
+            )
+
+        pick_a(0)
+        woven = {}
+        for n in range(len(steps)):
+            join(n)
+            if n == 0:
+                w1_q[0, 1] = quantize("w1_01", w1_round)
+                w1_round = round_w1(w1_raw[1, 1])
+                w3.append(deal("w3_1", w3_raw[1], U32))
+                d_win[2] = d_rows(2)
+            if n == 1:
+                w1_q[1, 1] = quantize("w1_11", w1_round)
+                d_win[3] = d_rows(3)
+            if 1 <= n <= 4:
+                a_win[n + 3] = a_rows(n + 3)
+            if 2 <= n <= 5:
+                d_win[n + 2] = d_rows(n + 2)
+            if n + 1 < len(steps):
+                pick_a(n + 1)
+            if n >= 1:
+                multiply(n - 1)
+            if n == 5:
+                z_q[0] = quantize("z0", weave(nc.scalar.copy, z_planes[0]))
+            if n in (6, 7):
+                w4_q[n - 6] = quantize("w4_%d" % (n - 6), round_w4(w4_raw[n - 6]))
+            if n == 8:
+                last_pass(0, 0)
+                woven[0] = weave(nc.scalar.copy, z_planes[1])
+            if n == 9:
+                z_q[1] = quantize("z1", woven[0])
+                last_pass(0, 1)
+            if n == 10:
+                add_base(0)
+                last_pass(1, 0)
+                woven[1] = weave(nc.scalar.copy, y_half[0])
+        multiply(len(steps) - 1)
+        y_planes(0, woven[1])
+        z_q[2] = quantize("z2", weave(nc.vector.tensor_copy, z_planes[2]))
+        last_pass(1, 1)
+        add_base(1)
+        y_planes(1, weave(nc.vector.tensor_copy, y_half[1]))
+        for q in range(4):
+            queue = nc.sync if q % 2 == 0 else nc.scalar
+            queue.dma_start(out_2[0, 4 * q : 4 * q + 4, :].bitcast(I32), y_scales[32 * q : 32 * q + 4, :].bitcast(I32))

@@ -24,6 +24,20 @@ PASS = 512
 BANK = 512
 HALF = J // 2
 
+PLACES = {
+    "v2_raw": 0, "v2_scale": 0, "w2_scale": 1, "w2": 6, "w1_rounded10": 6, "v3_1": 6,
+    "v_raw0": 10, "w1_raw11": 10,
+    "w1_raw00": 18, "w4_raw0": 18,
+    "v_raw1": 26, "v3_scale": 26, "w1_00_codes": 27, "w3_scale": 29, "w3_raw1": 30,
+    "v3_raw0": 34, "w4_raw1": 34,
+    "v3_raw1": 42, "w3_0": 42,
+    "w1_raw10": 50, "base_sb": 50,
+    "w1_rounded00": 58, "v3_plane": 62, "v3_0": 60,
+    "b1": 66, "w1_rounded01": 64, "w3_1": 84, "b0": 84,
+    "b2": 72, "w1_rounded11": 68, "w4_rounded1": 72,
+    "b3": 76, "w4_rounded0": 76,
+}
+
 
 def tile_list_diamond_report_features_kernel(
     tc, tab_words, tab_scales, tab2_words, tab2_scales, tab3_words, tab3_scales,
@@ -33,14 +47,15 @@ def tile_list_diamond_report_features_kernel(
     nc = tc.nc
     with ExitStack() as ctx:
         held = ctx.enter_context(tc.tile_pool(name="held", bufs=1))
-        stage = ctx.enter_context(tc.tile_pool(name="stage", bufs=5))
+        shared = ctx.enter_context(tc.tile_pool(name="shared", bufs=1))
         rounded = ctx.enter_context(tc.tile_pool(name="rounded", bufs=3))
         rows = ctx.enter_context(tc.tile_pool(name="rows", bufs=4))
         picked = ctx.enter_context(tc.tile_pool(name="picked", bufs=3))
-        first_psum = ctx.enter_context(tc.psum_pool(name="first_psum", bufs=4))
-        last_psum = ctx.enter_context(tc.psum_pool(name="last_psum", bufs=4))
+        psum = ctx.enter_context(tc.psum_pool(name="psum", bufs=8))
 
         def keep(name, shape, dtype):
+            if name in PLACES:
+                return shared.tile(shape, dtype, name=name, align_bytes=64, offset=PLACES[name] * 1024)
             return held.tile(shape, dtype, name=name, align_bytes=64)
 
         def load_list(name, src):
@@ -53,16 +68,16 @@ def tile_list_diamond_report_features_kernel(
             nc.vector.memset(plane[:].bitcast(I32), 0)
             return plane
 
-        def load_scales(queue, plane, src):
+        def load_scales(queue, plane, src, row=0):
             passes = src.shape[0]
             for q in range(4):
                 queue.dma_start(
-                    plane[32 * q : 32 * q + 4 * passes, :].bitcast(I32),
+                    plane[32 * q + row : 32 * q + row + 4 * passes, :].bitcast(I32),
                     src[:, 4 * q : 4 * q + 4, :].bitcast(I32),
                 )
 
-        def load_words(src, kp):
-            tile = stage.tile([P, T], I32, name="staged", align_bytes=64)
+        def load_words(name, src, kp):
+            tile = keep(name, [P, T], I32)
             nc.sync.dma_start(tile[:], src[kp].rearrange("p n i -> p (n i)").bitcast(I32))
             return tile
 
@@ -86,13 +101,14 @@ def tile_list_diamond_report_features_kernel(
             return out
 
         def load_w1(kp, a):
-            tile = stage.tile([P, 4, PASS], F32, name="staged", align_bytes=64)
+            tile = keep("w1_raw%d%d" % (kp, a), [P, 4, PASS], F32)
             src = w1[PASS * kp : PASS * (kp + 1), PASS * a : PASS * (a + 1)]
             nc.sync.dma_start(tile[:], src.rearrange("(p j) c -> p j c", j=4))
             return tile
 
-        def round_w1(raw):
-            out = rounded.tile([P, 4 * PASS], BF16, name="rounded", align_bytes=64)
+        def round_w1(kp, a):
+            raw = w1_raw[kp, a]
+            out = keep("w1_rounded%d%d" % (kp, a), [P, 4 * PASS], BF16)
             nc.scalar.copy(
                 out[:].rearrange("p (t g i j) -> p t g i j", t=4, g=16, i=8),
                 raw[:].rearrange("p j (g t i) -> p t g i j", t=4, g=16),
@@ -106,14 +122,15 @@ def tile_list_diamond_report_features_kernel(
             return tile
 
         def load_w4(a):
-            tile = stage.tile([P, 4, N], F32, name="staged", align_bytes=64)
+            tile = keep("w4_raw%d" % a, [P, 4, N], F32)
             src = w4[PASS * a : PASS * (a + 1), :].rearrange("(g t i) n -> t g i n", t=4, i=8)
             for t in range(4):
                 nc.sync.dma_start(tile[:, t, :], src[t])
             return tile
 
-        def round_w4(raw):
-            out = rounded.tile([P, 4 * N], BF16, name="rounded", align_bytes=64)
+        def round_w4(a):
+            raw = w4_raw[a]
+            out = keep("w4_rounded%d" % a, [P, 4 * N], BF16)
             nc.scalar.copy(
                 out[:].rearrange("p (u m t) -> p m u t", u=4, t=4),
                 raw[:].rearrange("p t (m u) -> p m u t", u=4),
@@ -130,7 +147,7 @@ def tile_list_diamond_report_features_kernel(
         def product_rows(tile, passes):
             for c in range(S // BANK):
                 cols = slice(BANK * c, BANK * (c + 1))
-                bank = first_psum.tile([P, BANK], F32, name="bank")
+                bank = psum.tile([P, BANK], F32, name="bank")
                 for n, (lhs, lhs_scale, rhs, rhs_scale) in enumerate(passes):
                     nc.tensor.matmul_mx(
                         out=bank[:], lhsT=lhs, lhsT_scale=lhs_scale,
@@ -141,44 +158,42 @@ def tile_list_diamond_report_features_kernel(
             return tile
 
         v2_plane = zeroed_plane("v2_plane", T)
-        w2_plane = zeroed_plane("w2_plane", H)
         v_plane = zeroed_plane("v_plane", T)
+        w2_plane = zeroed_plane("w2_plane", H)
         v3_plane = zeroed_plane("v3_plane", T)
         w3_plane = zeroed_plane("w3_plane", H)
 
         idx2 = load_list("idx2", offs2)
-        v2_raw = load_words(tab2_words, 0)
+        v2_raw = load_words("v2_raw", tab2_words, 0)
         load_scales(nc.sync, v2_plane, tab2_scales)
-        w1_raw = {(0, 0): load_w1(0, 0)}
+        load_scales(nc.gpsimd, v_plane, tab_scales, 8)
         w2_raw = keep("w2_raw", [P, 2 * H], U8)
         nc.sync.dma_start(w2_raw[:].bitcast(I32), w2_words[0].bitcast(I32))
+        w1_raw = {(0, 0): load_w1(0, 0)}
         load_scales(nc.sync, w2_plane, w2_scales)
-        v_raw = [load_words(tab_words, 0)]
         idx = load_list("idx", offs)
-        v_raw.append(load_words(tab_words, 1))
-        load_scales(nc.sync, v_plane, tab_scales)
-        w1_raw[1, 0] = load_w1(1, 0)
+        v_raw = [load_words("v_raw%d" % kp, tab_words, kp) for kp in range(2)]
         idx3 = load_list("idx3", offs3)
+        w1_raw[1, 0] = load_w1(1, 0)
+        load_scales(nc.sync, v3_plane, tab3_scales)
+        load_scales(nc.sync, w3_plane, w3_scales)
+        v3_raw = [load_words("v3_raw%d" % kp, tab3_words, kp) for kp in range(2)]
+        w3_raw = [load_w3(0)]
+        p1 = load_list("p1", pos1)
+        p2 = load_list("p2", pos2)
+        p3 = load_list("p3", pos3)
 
         v2 = gather_words("v2", v2_raw, idx2)
         v2_scale = gather_scales("v2_scale", v2_plane, idx2)
         w2_scale = deal("w2_scale", w2_plane, U8)
         w2 = deal("w2", w2_raw, U8)
-
-        v3_raw = [load_words(tab3_words, 0)]
-        load_scales(nc.sync, v3_plane, tab3_scales)
-        v = [gather_words("v_%d" % kp, v_raw[kp], idx) for kp in range(2)]
-        v3_raw.append(load_words(tab3_words, 1))
-        load_scales(nc.sync, w3_plane, w3_scales)
-        w3_raw = [load_w3(0)]
-        p1 = load_list("p1", pos1)
-        p2 = load_list("p2", pos2)
-        p3 = load_list("p3", pos3)
         v_scale = gather_scales("v_scale", v_plane, idx)
+        v = [gather_words("v_%d" % kp, v_raw[kp], idx) for kp in range(2)]
+        v3_scale = gather_scales("v3_scale", v3_plane, idx3)
 
         w1_q = {}
         for kp in range(2):
-            w1_q[kp, 0] = quantize("w1_%d0" % kp, round_w1(w1_raw[kp, 0]))
+            w1_q[kp, 0] = quantize("w1_%d0" % kp, round_w1(kp, 0))
             w1_raw[kp, 1] = load_w1(kp, 1)
         w3_raw.append(load_w3(1))
 
@@ -194,7 +209,7 @@ def tile_list_diamond_report_features_kernel(
             cols = slice(P * t, P * (t + 1))
             tile = rows.tile([P, S], F32, name="a_rows")
             return product_rows(tile, [
-                (w1_q[kp, a][0][:, cols].bitcast(FP8X4), w1_q[kp, a][1][:, cols], v[kp], v_scale[4 * kp : P, :])
+                (w1_q[kp, a][0][:, cols].bitcast(FP8X4), w1_q[kp, a][1][:, cols], v[kp], v_scale[8 + 4 * kp : P, :])
                 for kp in range(2)
             ])
 
@@ -210,6 +225,7 @@ def tile_list_diamond_report_features_kernel(
             ])
 
         b_win = [b_rows(s) for s in range(8)]
+        a_win = {s: a_rows(s) for s in range(3)}
 
         identity = keep("identity", [P, P], F32)
         make_identity(nc, identity[:])
@@ -220,13 +236,12 @@ def tile_list_diamond_report_features_kernel(
                 gain_rows[4 * a : 4 * a + 4, :].rearrange("t (g i) -> t g i", i=8),
                 gain[PASS * a : PASS * (a + 1)].rearrange("(g t i) -> t g i", t=4, i=8),
             )
-        gain_bank = first_psum.tile([P, P], F32, name="bank")
+        gain_bank = psum.tile([P, P], F32, name="bank")
         nc.tensor.transpose(gain_bank[:], gain_rows[:], identity[:])
         gain_cols = keep("gain_cols", [P, 8], F32)
         nc.scalar.copy(gain_cols[:], gain_bank[:, 0:8])
 
         v3 = [gather_words("v3_%d" % kp, v3_raw[kp], idx3) for kp in range(2)]
-        v3_scale = gather_scales("v3_scale", v3_plane, idx3)
         w3_scale = deal("w3_scale", w3_plane, U8)
         w3 = [deal("w3_0", w3_raw[0], U32)]
 
@@ -234,117 +249,94 @@ def tile_list_diamond_report_features_kernel(
         base_sb = keep("base_sb", [P, 4, J], F32)
         nc.sync.dma_start(base_sb[:], base.rearrange("(p u) j -> p u j", u=4))
 
-        a_win = {s: a_rows(s) for s in range(4)}
-        w1_round = round_w1(w1_raw[0, 1])
         d_win = {s: d_rows(s) for s in range(2)}
 
-        steps = [(s, 0, J) for s in range(4)]
-        steps = steps + [(s, HALF * h, HALF) for h in range(2) for s in range(4, 8)]
-        z_planes = {}
+        z_planes = [keep("z_planes%d" % a, [P, 4, J], BF16) for a in range(2)]
         a1, lit, dev = {}, {}, {}
 
-        def pick_a(n):
-            s, j0, width = steps[n]
-            a1[n] = picked.tile([P, width], F32, name="a1", bufs=2)
-            nc.vector.tensor_copy(a1[n][:], a_win[s][:].indirect(p1[:, j0 // 16 : (j0 + width) // 16]))
+        def pick_a(s):
+            a1[s] = picked.tile([P, J], F32, name="a1", bufs=2)
+            nc.vector.tensor_copy(a1[s][:], a_win[s][:].indirect(p1[:]))
 
-        def join(n):
-            s, j0, width = steps[n]
-            cols = slice(j0 // 16, (j0 + width) // 16)
-            lit[n] = picked.tile([P, width], F32, name="lit")
-            nc.vector.tensor_tensor(lit[n][:], b_win[s][:].indirect(p2[:, cols]), a1[n][:], ADD)
-            nc.scalar.activation(lit[n][:], lit[n][:], TANH)
-            dev[n] = picked.tile([P, width], F32, name="dev")
-            nc.vector.tensor_tensor(dev[n][:], d_win[s][:].indirect(p3[:, cols]), a1[n][:], SUBTRACT)
-            nc.scalar.activation(dev[n][:], dev[n][:], TANH, scale=-1.0)
+        def join(s):
+            lit[s] = picked.tile([P, J], F32, name="lit", bufs=3)
+            nc.vector.tensor_tensor(lit[s][:], b_win[s][:].indirect(p2[:]), a1[s][:], ADD)
+            dev[s] = picked.tile([P, J], F32, name="dev", bufs=3)
+            nc.vector.tensor_tensor(dev[s][:], d_win[s][:].indirect(p3[:]), a1[s][:], SUBTRACT)
 
-        def multiply(n):
-            s, j0, width = steps[n]
-            group = n // 4
-            if group not in z_planes:
-                z_planes[group] = keep("z_planes%d" % group, [P, 4, width], BF16)
+        def squash(s):
+            nc.scalar.activation(lit[s][:], lit[s][:], TANH)
+            nc.scalar.activation(dev[s][:], dev[s][:], TANH, scale=-1.0)
+
+        def multiply(s):
             nc.vector.scalar_tensor_tensor(
-                z_planes[group][:, s % 4, :], lit[n][:], gain_cols[:, s : s + 1], dev[n][:], MULT, MULT
+                z_planes[s // 4][:, s % 4, :], lit[s][:], gain_cols[:, s : s + 1], dev[s][:], MULT, MULT
             )
 
         def weave(engine_copy, planes):
             width = planes.shape[2]
             out = rounded.tile([P, 4 * width], BF16, name="rounded", align_bytes=64)
-            engine_copy(out[:].rearrange("p (j t) -> p j t", t=4), planes[:].rearrange("p t j -> p j t"))
+            engine_copy(out[:].rearrange("p (j t) -> p j t", t=4), planes.rearrange("p t j -> p j t"))
             return out
 
         y_codes = keep("y_codes", [P, J], U32)
         y_scales = keep("y_scales", [P, J], U8)
-        w4_q, z_q, y_banks, y_half = {}, {}, {}, {}
+        w4_q = {}
 
-        def last_pass(h, a):
-            codes, scales = z_q[a * (1 + h)]
-            j0 = HALF * h * (1 - a)
-            for u in range(4):
-                if a == 0:
-                    y_banks[h, u] = last_psum.tile([P, HALF], F32, name="y_bank")
-                nc.tensor.matmul_mx(
-                    out=y_banks[h, u][:],
-                    lhsT=w4_q[a][0][:, P * u : P * (u + 1)].bitcast(FP8X4),
-                    lhsT_scale=w4_q[a][1][:, P * u : P * (u + 1)],
-                    rhs=codes[:, j0 : j0 + HALF].bitcast(FP8X4), rhs_scale=scales[:, j0 : j0 + HALF],
-                    start=(a == 0), stop=(a == 1),
-                )
-
-        def add_base(h):
-            cols = slice(HALF * h, HALF * (h + 1))
-            y_half[h] = keep("y%d" % h, [P, 4, HALF], F32)
-            for u in range(4):
-                nc.vector.tensor_tensor(y_half[h][:, u, :], y_banks[h, u][:], base_sb[:, u, cols], ADD)
-            nc.sync.dma_start(out_0.rearrange("(p u) j -> p u j", u=4)[:, :, cols], y_half[h][:])
-
-        def y_planes(h, woven):
-            cols = slice(HALF * h, HALF * (h + 1))
-            nc.vector.quantize_mx(out=y_codes[:, cols].bitcast(FP8X4), scales=y_scales[:, cols], in_=woven[:])
-            nc.scalar.dma_start(
-                out_1[0].rearrange("p m t -> p (m t)").bitcast(I32)[:, cols], y_codes[:, cols].bitcast(I32)
+        def last_pass(out, u, a, z_q, start, stop):
+            nc.tensor.matmul_mx(
+                out=out,
+                lhsT=w4_q[a][0][:, P * u : P * (u + 1)].bitcast(FP8X4),
+                lhsT_scale=w4_q[a][1][:, P * u : P * (u + 1)],
+                rhs=z_q[0][:].bitcast(FP8X4), rhs_scale=z_q[1][:],
+                start=start, stop=stop,
             )
 
         pick_a(0)
-        woven = {}
-        for n in range(len(steps)):
-            join(n)
-            if n == 0:
-                w1_q[0, 1] = quantize("w1_01", w1_round)
-                w1_round = round_w1(w1_raw[1, 1])
+        for s in range(8):
+            join(s)
+            if s == 0:
                 w3.append(deal("w3_1", w3_raw[1], U32))
-                d_win[2] = d_rows(2)
-            if n == 1:
-                w1_q[1, 1] = quantize("w1_11", w1_round)
-                d_win[3] = d_rows(3)
-            if 1 <= n <= 4:
-                a_win[n + 3] = a_rows(n + 3)
-            if 2 <= n <= 5:
-                d_win[n + 2] = d_rows(n + 2)
-            if n + 1 < len(steps):
-                pick_a(n + 1)
-            if n >= 1:
-                multiply(n - 1)
-            if n == 5:
-                z_q[0] = quantize("z0", weave(nc.scalar.copy, z_planes[0]))
-            if n in (6, 7):
-                w4_q[n - 6] = quantize("w4_%d" % (n - 6), round_w4(w4_raw[n - 6]))
-            if n == 8:
-                last_pass(0, 0)
-                woven[0] = weave(nc.scalar.copy, z_planes[1])
-            if n == 9:
-                z_q[1] = quantize("z1", woven[0])
-                last_pass(0, 1)
-            if n == 10:
-                add_base(0)
-                last_pass(1, 0)
-                woven[1] = weave(nc.scalar.copy, y_half[0])
-        multiply(len(steps) - 1)
-        y_planes(0, woven[1])
-        z_q[2] = quantize("z2", weave(nc.vector.tensor_copy, z_planes[2]))
-        last_pass(1, 1)
-        add_base(1)
-        y_planes(1, weave(nc.vector.tensor_copy, y_half[1]))
+            if s < 2:
+                w1_q[s, 1] = quantize("w1_%d1" % s, round_w1(s, 1))
+            if s < 5:
+                a_win[s + 3] = a_rows(s + 3)
+            if s < 6:
+                d_win[s + 2] = d_rows(s + 2)
+            squash(s)
+            if s < 7:
+                pick_a(s + 1)
+            if s >= 1:
+                multiply(s - 1)
+            if s in (4, 4 + 1):
+                w4_q[s - 4] = quantize("w4_%d" % (s - 4), round_w4(s - 4))
+            if s == 5:
+                z0_q = quantize("z0", weave(nc.vector.tensor_copy, z_planes[0][:]))
+        multiply(7)
+
+        halves = [slice(HALF * h, HALF * (h + 1)) for h in range(2)]
+        y_banks = [psum.tile([P, J], F32, name="bank") for u in range(4)]
+        for u in range(4):
+            last_pass(y_banks[u][:], u, 0, z0_q, True, False)
+        woven = [weave(nc.vector.tensor_copy, z_planes[1][:, :, cols]) for cols in halves]
+        for h in range(2):
+            z1_q = quantize("z1_%d" % h, woven[h])
+            for u in range(4):
+                last_pass(y_banks[u][:, halves[h]], u, 1, z1_q, False, h == 1)
+        y = keep("y", [P, 4, J], F32)
+        y_rows = out_0.rearrange("(p u) j -> p u j", u=4)
+        for u in range(4):
+            nc.vector.tensor_tensor(y[:, u, :], y_banks[u][:], base_sb[:, u, :], ADD)
+            if u % 2 == 1:
+                nc.sync.dma_start(y_rows[:, u - 1 : u + 1, :], y[:, u - 1 : u + 1, :])
+        y_woven = [
+            weave(engine_copy, y[:, :, cols])
+            for engine_copy, cols in zip((nc.vector.tensor_copy, nc.scalar.copy), halves)
+        ]
+        for h in range(2):
+            cols = halves[h]
+            nc.vector.quantize_mx(out=y_codes[:, cols].bitcast(FP8X4), scales=y_scales[:, cols], in_=y_woven[h][:])
+        nc.sync.dma_start(out_1[0].rearrange("p m t -> p (m t)").bitcast(I32), y_codes[:].bitcast(I32))
         for q in range(4):
             queue = nc.sync if q % 2 == 0 else nc.scalar
             queue.dma_start(out_2[0, 4 * q : 4 * q + 4, :].bitcast(I32), y_scales[32 * q : 32 * q + 4, :].bitcast(I32))

@@ -22,7 +22,12 @@ TANH = mybir.ActivationFunctionType.Tanh
 P = 128
 PASS = 512
 BANK = 512
-HALF = J // 2
+SLICES = H // P
+V_ROW0 = 8
+A_AHEAD = 3
+D_AHEAD = 2
+W4_AT = 4
+Z0_AT = 5
 
 PLACES = {
     "v2_raw": 0, "v2_scale": 0, "w2_scale": 1, "w2": 6, "w1_rounded10": 6, "v3_1": 6,
@@ -33,7 +38,7 @@ PLACES = {
     "v3_raw1": 42, "w3_0": 42,
     "w1_raw10": 50, "base_sb": 50,
     "w1_rounded00": 58, "v3_plane": 62, "v3_0": 60,
-    "b1": 66, "w1_rounded01": 64, "w3_1": 84, "b0": 84,
+    "b1": 66, "w1_rounded01": 82, "w3_1": 86, "b0": 84,
     "b2": 72, "w1_rounded11": 68, "w4_rounded1": 72,
     "b3": 76, "w4_rounded0": 76,
 }
@@ -68,72 +73,69 @@ def tile_list_diamond_report_features_kernel(
             nc.vector.memset(plane[:].bitcast(I32), 0)
             return plane
 
-        def load_scales(queue, plane, src, row=0):
+        def load_scales(queue, plane, src, row0=0):
             passes = src.shape[0]
             for q in range(4):
                 queue.dma_start(
-                    plane[32 * q + row : 32 * q + row + 4 * passes, :].bitcast(I32),
+                    plane[32 * q + row0 : 32 * q + row0 + 4 * passes, :].bitcast(I32),
                     src[:, 4 * q : 4 * q + 4, :].bitcast(I32),
                 )
 
         def load_words(name, src, kp):
             tile = keep(name, [P, T], I32)
-            nc.sync.dma_start(tile[:], src[kp].rearrange("p n i -> p (n i)").bitcast(I32))
+            nc.sync.dma_start(tile[:], src[kp].rearrange("p c j -> p (c j)").bitcast(I32))
             return tile
 
-        def gather_words(name, window, idx):
+        def gather_words(name, window, offsets):
             out = keep(name, [P, S], U32)
-            nc.vector.tensor_copy(out[:], window[:].bitcast(U32).indirect(idx[:]))
+            nc.vector.tensor_copy(out[:], window[:].bitcast(U32).indirect(offsets[:]))
             return out
 
-        def gather_scales(name, window, idx):
+        def gather_scales(name, window, offsets):
             out = keep(name, [P, S], U8)
-            nc.vector.tensor_copy(out[:], window[:].indirect(idx[:]))
+            nc.vector.tensor_copy(out[:], window[:].indirect(offsets[:]))
             return out
 
         def deal(name, src, dtype):
             out = keep(name, list(src.shape), dtype)
-            words = src[:].bitcast(I32)
             nc.vector.tensor_copy(
-                out[:].bitcast(I32).rearrange("p (a t g w) -> p a t g w", a=2, t=4, g=16),
-                words.rearrange("p (a g t w) -> p a t g w", a=2, t=4, g=16),
+                out[:].bitcast(I32).rearrange("p (part t g w) -> p part t g w", part=2, t=4, g=16),
+                src[:].bitcast(I32).rearrange("p (part g t w) -> p part t g w", part=2, t=4, g=16),
             )
             return out
 
-        def load_w1(kp, a):
-            tile = keep("w1_raw%d%d" % (kp, a), [P, 4, PASS], F32)
-            src = w1[PASS * kp : PASS * (kp + 1), PASS * a : PASS * (a + 1)]
+        def load_w1(kp, half):
+            tile = keep("w1_raw%d%d" % (kp, half), [P, 4, PASS], F32)
+            src = w1[PASS * kp : PASS * (kp + 1), PASS * half : PASS * (half + 1)]
             nc.sync.dma_start(tile[:], src.rearrange("(p j) c -> p j c", j=4))
             return tile
 
-        def round_w1(kp, a):
-            raw = w1_raw[kp, a]
-            out = keep("w1_rounded%d%d" % (kp, a), [P, 4 * PASS], BF16)
+        def round_w1(kp, half):
+            out = keep("w1_rounded%d%d" % (kp, half), [P, 4 * PASS], BF16)
             nc.scalar.copy(
                 out[:].rearrange("p (t g i j) -> p t g i j", t=4, g=16, i=8),
-                raw[:].rearrange("p j (g t i) -> p t g i j", t=4, g=16),
+                w1_raw[kp, half][:].rearrange("p j (g t i) -> p t g i j", t=4, g=16),
             )
             return out
 
-        def load_w3(a):
-            tile = keep("w3_raw%d" % a, [P, 2 * PASS], I32)
-            src = w3_words[:, :, PASS * a : PASS * (a + 1), :].rearrange("k p n i -> p k (n i)")
-            nc.sync.dma_start(tile[:].rearrange("p (k n) -> p k n", k=2), src.bitcast(I32))
+        def load_w3(half):
+            tile = keep("w3_raw%d" % half, [P, 2 * PASS], I32)
+            src = w3_words[:, :, PASS * half : PASS * (half + 1), :].rearrange("kp p c j -> p kp (c j)")
+            nc.sync.dma_start(tile[:].rearrange("p (kp c) -> p kp c", kp=2), src.bitcast(I32))
             return tile
 
-        def load_w4(a):
-            tile = keep("w4_raw%d" % a, [P, 4, N], F32)
-            src = w4[PASS * a : PASS * (a + 1), :].rearrange("(g t i) n -> t g i n", t=4, i=8)
+        def load_w4(half):
+            tile = keep("w4_raw%d" % half, [P, 4, N], F32)
+            src = w4[PASS * half : PASS * (half + 1), :].rearrange("(g t i) n -> t g i n", t=4, i=8)
             for t in range(4):
                 nc.sync.dma_start(tile[:, t, :], src[t])
             return tile
 
-        def round_w4(a):
-            raw = w4_raw[a]
-            out = keep("w4_rounded%d" % a, [P, 4 * N], BF16)
+        def round_w4(half):
+            out = keep("w4_rounded%d" % half, [P, 4 * N], BF16)
             nc.scalar.copy(
                 out[:].rearrange("p (u m t) -> p m u t", u=4, t=4),
-                raw[:].rearrange("p t (m u) -> p m u t", u=4),
+                w4_raw[half][:].rearrange("p t (m u) -> p m u t", u=4),
             )
             return out
 
@@ -145,14 +147,14 @@ def tile_list_diamond_report_features_kernel(
             return codes, scales
 
         def product_rows(tile, passes):
-            for c in range(S // BANK):
-                cols = slice(BANK * c, BANK * (c + 1))
+            for c0 in range(0, S, BANK):
+                cols = slice(c0, c0 + BANK)
                 bank = psum.tile([P, BANK], F32, name="bank")
-                for n, (lhs, lhs_scale, rhs, rhs_scale) in enumerate(passes):
+                for kp, (lhs, lhs_scale, rhs, rhs_scale) in enumerate(passes):
                     nc.tensor.matmul_mx(
                         out=bank[:], lhsT=lhs, lhsT_scale=lhs_scale,
                         rhs=rhs[:, cols].bitcast(FP8X4), rhs_scale=rhs_scale[:, cols],
-                        start=(n == 0), stop=(n == len(passes) - 1),
+                        start=(kp == 0), stop=(kp == len(passes) - 1),
                     )
                 nc.scalar.copy(tile[:, cols], bank[:])
             return tile
@@ -166,7 +168,7 @@ def tile_list_diamond_report_features_kernel(
         idx2 = load_list("idx2", offs2)
         v2_raw = load_words("v2_raw", tab2_words, 0)
         load_scales(nc.sync, v2_plane, tab2_scales)
-        load_scales(nc.gpsimd, v_plane, tab_scales, 8)
+        load_scales(nc.gpsimd, v_plane, tab_scales, V_ROW0)
         w2_raw = keep("w2_raw", [P, 2 * H], U8)
         nc.sync.dma_start(w2_raw[:].bitcast(I32), w2_words[0].bitcast(I32))
         w1_raw = {(0, 0): load_w1(0, 0)}
@@ -175,7 +177,7 @@ def tile_list_diamond_report_features_kernel(
         v_raw = [load_words("v_raw%d" % kp, tab_words, kp) for kp in range(2)]
         idx3 = load_list("idx3", offs3)
         w1_raw[1, 0] = load_w1(1, 0)
-        load_scales(nc.sync, v3_plane, tab3_scales)
+        load_scales(nc.gpsimd, v3_plane, tab3_scales)
         load_scales(nc.sync, w3_plane, w3_scales)
         v3_raw = [load_words("v3_raw%d" % kp, tab3_words, kp) for kp in range(2)]
         w3_raw = [load_w3(0)]
@@ -205,53 +207,56 @@ def tile_list_diamond_report_features_kernel(
             )])
 
         def a_rows(s):
-            a, t = divmod(s, 4)
+            half, t = divmod(s, 4)
             cols = slice(P * t, P * (t + 1))
             tile = rows.tile([P, S], F32, name="a_rows")
             return product_rows(tile, [
-                (w1_q[kp, a][0][:, cols].bitcast(FP8X4), w1_q[kp, a][1][:, cols], v[kp], v_scale[8 + 4 * kp : P, :])
+                (
+                    w1_q[kp, half][0][:, cols].bitcast(FP8X4), w1_q[kp, half][1][:, cols],
+                    v[kp], v_scale[V_ROW0 + 4 * kp : P, :],
+                )
                 for kp in range(2)
             ])
 
         def d_rows(s):
-            a, t = divmod(s, 4)
+            half, t = divmod(s, 4)
             tile = rows.tile([P, S], F32, name="d_rows")
             return product_rows(tile, [
                 (
-                    w3[a][:, PASS * kp + P * t : PASS * kp + P * (t + 1)].bitcast(FP8X4),
+                    w3[half][:, PASS * kp + P * t : PASS * kp + P * (t + 1)].bitcast(FP8X4),
                     w3_scale[4 * kp : P, P * s : P * (s + 1)], v3[kp], v3_scale[4 * kp : P, :],
                 )
                 for kp in range(2)
             ])
 
-        b_win = [b_rows(s) for s in range(8)]
-        a_win = {s: a_rows(s) for s in range(3)}
+        b_win = [b_rows(s) for s in range(SLICES)]
+        a_win = {s: a_rows(s) for s in range(A_AHEAD)}
 
         identity = keep("identity", [P, P], F32)
         make_identity(nc, identity[:])
         gain_rows = keep("gain_rows", [P, P], F32)
         nc.gpsimd.memset(gain_rows[:], 0.0)
-        for a in range(2):
+        for half in range(2):
             nc.gpsimd.dma_start(
-                gain_rows[4 * a : 4 * a + 4, :].rearrange("t (g i) -> t g i", i=8),
-                gain[PASS * a : PASS * (a + 1)].rearrange("(g t i) -> t g i", t=4, i=8),
+                gain_rows[4 * half : 4 * half + 4, :].rearrange("t (g i) -> t g i", i=8),
+                gain[PASS * half : PASS * (half + 1)].rearrange("(g t i) -> t g i", t=4, i=8),
             )
         gain_bank = psum.tile([P, P], F32, name="bank")
         nc.tensor.transpose(gain_bank[:], gain_rows[:], identity[:])
-        gain_cols = keep("gain_cols", [P, 8], F32)
-        nc.scalar.copy(gain_cols[:], gain_bank[:, 0:8])
+        gain_cols = keep("gain_cols", [P, SLICES], F32)
+        nc.scalar.copy(gain_cols[:], gain_bank[:, 0:SLICES])
 
         v3 = [gather_words("v3_%d" % kp, v3_raw[kp], idx3) for kp in range(2)]
         w3_scale = deal("w3_scale", w3_plane, U8)
         w3 = [deal("w3_0", w3_raw[0], U32)]
 
-        w4_raw = [load_w4(a) for a in range(2)]
+        w4_raw = [load_w4(half) for half in range(2)]
         base_sb = keep("base_sb", [P, 4, J], F32)
-        nc.sync.dma_start(base_sb[:], base.rearrange("(p u) j -> p u j", u=4))
+        nc.sync.dma_start(base_sb[:], base.rearrange("(p u) c -> p u c", u=4))
 
-        d_win = {s: d_rows(s) for s in range(2)}
+        d_win = {s: d_rows(s) for s in range(D_AHEAD)}
 
-        z_planes = [keep("z_planes%d" % a, [P, 4, J], BF16) for a in range(2)]
+        z_slices = [keep("z_planes%d" % half, [P, 4, J], BF16) for half in range(2)]
         a1, lit, dev = {}, {}, {}
 
         def pick_a(s):
@@ -259,84 +264,83 @@ def tile_list_diamond_report_features_kernel(
             nc.vector.tensor_copy(a1[s][:], a_win[s][:].indirect(p1[:]))
 
         def join(s):
-            lit[s] = picked.tile([P, J], F32, name="lit", bufs=3)
+            lit[s] = picked.tile([P, J], F32, name="lit")
             nc.vector.tensor_tensor(lit[s][:], b_win[s][:].indirect(p2[:]), a1[s][:], ADD)
-            dev[s] = picked.tile([P, J], F32, name="dev", bufs=3)
+            dev[s] = picked.tile([P, J], F32, name="dev")
             nc.vector.tensor_tensor(dev[s][:], d_win[s][:].indirect(p3[:]), a1[s][:], SUBTRACT)
 
-        def squash(s):
+        def take_tanh(s):
             nc.scalar.activation(lit[s][:], lit[s][:], TANH)
             nc.scalar.activation(dev[s][:], dev[s][:], TANH, scale=-1.0)
 
         def multiply(s):
             nc.vector.scalar_tensor_tensor(
-                z_planes[s // 4][:, s % 4, :], lit[s][:], gain_cols[:, s : s + 1], dev[s][:], MULT, MULT
+                z_slices[s // 4][:, s % 4, :], lit[s][:], gain_cols[:, s : s + 1], dev[s][:], MULT, MULT
             )
 
-        def weave(engine_copy, planes):
-            width = planes.shape[2]
+        def weave(engine_copy, four_slices):
+            width = four_slices.shape[2]
             out = rounded.tile([P, 4 * width], BF16, name="rounded", align_bytes=64)
-            engine_copy(out[:].rearrange("p (j t) -> p j t", t=4), planes.rearrange("p t j -> p j t"))
+            engine_copy(out[:].rearrange("p (c t) -> p c t", t=4), four_slices.rearrange("p t c -> p c t"))
             return out
 
         y_codes = keep("y_codes", [P, J], U32)
         y_scales = keep("y_scales", [P, J], U8)
         w4_q = {}
 
-        def last_pass(out, u, a, z_q, start, stop):
+        def last_pass(out, u, half, z_q, start, stop):
             nc.tensor.matmul_mx(
                 out=out,
-                lhsT=w4_q[a][0][:, P * u : P * (u + 1)].bitcast(FP8X4),
-                lhsT_scale=w4_q[a][1][:, P * u : P * (u + 1)],
+                lhsT=w4_q[half][0][:, P * u : P * (u + 1)].bitcast(FP8X4),
+                lhsT_scale=w4_q[half][1][:, P * u : P * (u + 1)],
                 rhs=z_q[0][:].bitcast(FP8X4), rhs_scale=z_q[1][:],
                 start=start, stop=stop,
             )
 
         pick_a(0)
-        for s in range(8):
+        for s in range(SLICES):
             join(s)
             if s == 0:
                 w3.append(deal("w3_1", w3_raw[1], U32))
             if s < 2:
                 w1_q[s, 1] = quantize("w1_%d1" % s, round_w1(s, 1))
-            if s < 5:
-                a_win[s + 3] = a_rows(s + 3)
-            if s < 6:
-                d_win[s + 2] = d_rows(s + 2)
-            squash(s)
-            if s < 7:
+            if s + A_AHEAD < SLICES:
+                a_win[s + A_AHEAD] = a_rows(s + A_AHEAD)
+            if s + D_AHEAD < SLICES:
+                d_win[s + D_AHEAD] = d_rows(s + D_AHEAD)
+            take_tanh(s)
+            if s + 1 < SLICES:
                 pick_a(s + 1)
             if s >= 1:
                 multiply(s - 1)
-            if s in (4, 4 + 1):
-                w4_q[s - 4] = quantize("w4_%d" % (s - 4), round_w4(s - 4))
-            if s == 5:
-                z0_q = quantize("z0", weave(nc.vector.tensor_copy, z_planes[0][:]))
-        multiply(7)
+            if s in (W4_AT, W4_AT + 1):
+                w4_q[s - W4_AT] = quantize("w4_%d" % (s - W4_AT), round_w4(s - W4_AT))
+            if s == Z0_AT:
+                z0_q = quantize("z0", weave(nc.vector.tensor_copy, z_slices[0][:]))
+        multiply(SLICES - 1)
 
-        halves = [slice(HALF * h, HALF * (h + 1)) for h in range(2)]
+        parts = [slice(c0, c0 + J // 2) for c0 in (0, J // 2)]
+        copies = (nc.vector.tensor_copy, nc.scalar.copy)
         y_banks = [psum.tile([P, J], F32, name="bank") for u in range(4)]
         for u in range(4):
             last_pass(y_banks[u][:], u, 0, z0_q, True, False)
-        woven = [weave(nc.vector.tensor_copy, z_planes[1][:, :, cols]) for cols in halves]
-        for h in range(2):
-            z1_q = quantize("z1_%d" % h, woven[h])
+        z_woven = [weave(engine_copy, z_slices[1][:, :, cols]) for engine_copy, cols in zip(copies, parts)]
+        for n_part, cols in enumerate(parts):
+            z1_q = quantize("z1_%d" % n_part, z_woven[n_part])
             for u in range(4):
-                last_pass(y_banks[u][:, halves[h]], u, 1, z1_q, False, h == 1)
+                last_pass(y_banks[u][:, cols], u, 1, z1_q, False, n_part == len(parts) - 1)
         y = keep("y", [P, 4, J], F32)
-        y_rows = out_0.rearrange("(p u) j -> p u j", u=4)
+        y_out = out_0.rearrange("(p u) c -> p u c", u=4)
         for u in range(4):
             nc.vector.tensor_tensor(y[:, u, :], y_banks[u][:], base_sb[:, u, :], ADD)
             if u % 2 == 1:
-                nc.sync.dma_start(y_rows[:, u - 1 : u + 1, :], y[:, u - 1 : u + 1, :])
-        y_woven = [
-            weave(engine_copy, y[:, :, cols])
-            for engine_copy, cols in zip((nc.vector.tensor_copy, nc.scalar.copy), halves)
-        ]
-        for h in range(2):
-            cols = halves[h]
-            nc.vector.quantize_mx(out=y_codes[:, cols].bitcast(FP8X4), scales=y_scales[:, cols], in_=y_woven[h][:])
-        nc.sync.dma_start(out_1[0].rearrange("p m t -> p (m t)").bitcast(I32), y_codes[:].bitcast(I32))
+                nc.sync.dma_start(y_out[:, u - 1 : u + 1, :], y[:, u - 1 : u + 1, :])
+        y_woven = [weave(engine_copy, y[:, :, cols]) for engine_copy, cols in zip(copies, parts)]
+        for woven, cols in zip(y_woven, parts):
+            nc.vector.quantize_mx(out=y_codes[:, cols].bitcast(FP8X4), scales=y_scales[:, cols], in_=woven[:])
+        nc.sync.dma_start(out_1[0].rearrange("p c t -> p (c t)").bitcast(I32), y_codes[:].bitcast(I32))
         for q in range(4):
             queue = nc.sync if q % 2 == 0 else nc.scalar
-            queue.dma_start(out_2[0, 4 * q : 4 * q + 4, :].bitcast(I32), y_scales[32 * q : 32 * q + 4, :].bitcast(I32))
+            queue.dma_start(
+                out_2[0, 4 * q : 4 * q + 4, :].bitcast(I32), y_scales[32 * q : 32 * q + 4, :].bitcast(I32)
+            )

from contextlib import ExitStack

import concourse.mybir as mybir
from concourse.masks import make_identity

K, K2, H, N, T, S, J = 1024, 512, 1024, 512, 2048, 1024, 512
FLOPS = 2 * (K + K2 + K) * H * S + 2 * H * N * J

F32 = mybir.dt.float32
BF16 = mybir.dt.bfloat16
I32 = mybir.dt.int32
U32 = mybir.dt.uint32
U16 = mybir.dt.uint16
U8 = mybir.dt.uint8
FP8X4 = mybir.dt.float8_e4m3fn_x4
FP4X4 = mybir.dt.float4_e2m1fn_x4
MULT = mybir.AluOpType.mult
ADD = mybir.AluOpType.add
SUBTRACT = mybir.AluOpType.subtract
TANH = mybir.ActivationFunctionType.Tanh

P = 128
PASS = 512
BANK = 512
SLICES = H // P
V_ROW0 = 8
A_AHEAD = 3
D_AHEAD = 2
W4_AT = 4
Z0_AT = 5

PLACES = {
    "v2_raw": 0, "v2_scale": 0, "w2_scale": 1, "w2": 6, "w1_rounded10": 6, "v3_1": 6,
    "v_raw0": 10, "w1_raw11": 10,
    "w1_raw00": 18, "w4_raw0": 18,
    "v_raw1": 26, "v3_scale": 26, "w1_00_codes": 27, "w3_scale": 29, "w3_raw1": 30,
    "v3_raw0": 34, "w4_raw1": 34,
    "v3_raw1": 42, "w3_0": 42,
    "w1_raw10": 50, "base_sb": 50,
    "w1_rounded00": 58, "v3_plane": 62, "v3_0": 60,
    "b1": 66, "w1_rounded01": 82, "w3_1": 86, "b0": 84,
    "b2": 72, "w1_rounded11": 68, "w4_rounded1": 72,
    "b3": 76, "w4_rounded0": 76,
}


def tile_list_diamond_report_features_kernel(
    tc, tab_words, tab_scales, tab2_words, tab2_scales, tab3_words, tab3_scales,
    offs, offs2, offs3, pos1, pos2, pos3, w1, w2_words, w2_scales, w3_words, w3_scales,
    gain, w4, base, out_0, out_1, out_2,
):
    nc = tc.nc
    with ExitStack() as ctx:
        held = ctx.enter_context(tc.tile_pool(name="held", bufs=1))
        shared = ctx.enter_context(tc.tile_pool(name="shared", bufs=1))
        rounded = ctx.enter_context(tc.tile_pool(name="rounded", bufs=3))
        rows = ctx.enter_context(tc.tile_pool(name="rows", bufs=4))
        picked = ctx.enter_context(tc.tile_pool(name="picked", bufs=3))
        psum = ctx.enter_context(tc.psum_pool(name="psum", bufs=8))

        def keep(name, shape, dtype):
            if name in PLACES:
                return shared.tile(shape, dtype, name=name, align_bytes=64, offset=PLACES[name] * 1024)
            return held.tile(shape, dtype, name=name, align_bytes=64)

        def load_list(name, src):
            tile = held.tile(list(src.shape), U16, name=name)
            nc.sync.dma_start(tile[:], src)
            return tile

        def zeroed_plane(name, width):
            plane = keep(name, [P, width], U8)
            nc.vector.memset(plane[:].bitcast(I32), 0)
            return plane

        def load_scales(queue, plane, src, row0=0):
            passes = src.shape[0]
            for q in range(4):
                queue.dma_start(
                    plane[32 * q + row0 : 32 * q + row0 + 4 * passes, :].bitcast(I32),
                    src[:, 4 * q : 4 * q + 4, :].bitcast(I32),
                )

        def load_words(name, src, kp):
            tile = keep(name, [P, T], I32)
            nc.sync.dma_start(tile[:], src[kp].rearrange("p c j -> p (c j)").bitcast(I32))
            return tile

        def gather_words(name, window, offsets):
            out = keep(name, [P, S], U32)
            nc.vector.tensor_copy(out[:], window[:].bitcast(U32).indirect(offsets[:]))
            return out

        def gather_scales(name, window, offsets):
            out = keep(name, [P, S], U8)
            nc.vector.tensor_copy(out[:], window[:].indirect(offsets[:]))
            return out

        def deal(name, src, dtype):
            out = keep(name, list(src.shape), dtype)
            nc.vector.tensor_copy(
                out[:].bitcast(I32).rearrange("p (part t g w) -> p part t g w", part=2, t=4, g=16),
                src[:].bitcast(I32).rearrange("p (part g t w) -> p part t g w", part=2, t=4, g=16),
            )
            return out

        def load_w1(kp, half):
            tile = keep("w1_raw%d%d" % (kp, half), [P, 4, PASS], F32)
            src = w1[PASS * kp : PASS * (kp + 1), PASS * half : PASS * (half + 1)]
            nc.sync.dma_start(tile[:], src.rearrange("(p j) c -> p j c", j=4))
            return tile

        def round_w1(kp, half):
            out = keep("w1_rounded%d%d" % (kp, half), [P, 4 * PASS], BF16)
            nc.scalar.copy(
                out[:].rearrange("p (t g i j) -> p t g i j", t=4, g=16, i=8),
                w1_raw[kp, half][:].rearrange("p j (g t i) -> p t g i j", t=4, g=16),
            )
            return out

        def load_w3(half):
            tile = keep("w3_raw%d" % half, [P, 2 * PASS], I32)
            src = w3_words[:, :, PASS * half : PASS * (half + 1), :].rearrange("kp p c j -> p kp (c j)")
            nc.sync.dma_start(tile[:].rearrange("p (kp c) -> p kp c", kp=2), src.bitcast(I32))
            return tile

        def load_w4(half):
            tile = keep("w4_raw%d" % half, [P, 4, N], F32)
            src = w4[PASS * half : PASS * (half + 1), :].rearrange("(g t i) n -> t g i n", t=4, i=8)
            for t in range(4):
                nc.sync.dma_start(tile[:, t, :], src[t])
            return tile

        def round_w4(half):
            out = keep("w4_rounded%d" % half, [P, 4 * N], BF16)
            nc.scalar.copy(
                out[:].rearrange("p (u m t) -> p m u t", u=4, t=4),
                w4_raw[half][:].rearrange("p t (m u) -> p m u t", u=4),
            )
            return out

        def quantize(name, values):
            width = values.shape[1] // 4
            codes = keep(name + "_codes", [P, width], U32)
            scales = keep(name + "_scales", [P, width], U8)
            nc.vector.quantize_mx(out=codes[:].bitcast(FP8X4), scales=scales[:], in_=values[:])
            return codes, scales

        def product_rows(tile, passes):
            for c0 in range(0, S, BANK):
                cols = slice(c0, c0 + BANK)
                bank = psum.tile([P, BANK], F32, name="bank")
                for kp, (lhs, lhs_scale, rhs, rhs_scale) in enumerate(passes):
                    nc.tensor.matmul_mx(
                        out=bank[:], lhsT=lhs, lhsT_scale=lhs_scale,
                        rhs=rhs[:, cols].bitcast(FP8X4), rhs_scale=rhs_scale[:, cols],
                        start=(kp == 0), stop=(kp == len(passes) - 1),
                    )
                nc.scalar.copy(tile[:, cols], bank[:])
            return tile

        v2_plane = zeroed_plane("v2_plane", T)
        v_plane = zeroed_plane("v_plane", T)
        w2_plane = zeroed_plane("w2_plane", H)
        v3_plane = zeroed_plane("v3_plane", T)
        w3_plane = zeroed_plane("w3_plane", H)

        idx2 = load_list("idx2", offs2)
        v2_raw = load_words("v2_raw", tab2_words, 0)
        load_scales(nc.sync, v2_plane, tab2_scales)
        load_scales(nc.gpsimd, v_plane, tab_scales, V_ROW0)
        w2_raw = keep("w2_raw", [P, 2 * H], U8)
        nc.sync.dma_start(w2_raw[:].bitcast(I32), w2_words[0].bitcast(I32))
        w1_raw = {(0, 0): load_w1(0, 0)}
        load_scales(nc.sync, w2_plane, w2_scales)
        idx = load_list("idx", offs)
        v_raw = [load_words("v_raw%d" % kp, tab_words, kp) for kp in range(2)]
        idx3 = load_list("idx3", offs3)
        w1_raw[1, 0] = load_w1(1, 0)
        load_scales(nc.gpsimd, v3_plane, tab3_scales)
        load_scales(nc.sync, w3_plane, w3_scales)
        v3_raw = [load_words("v3_raw%d" % kp, tab3_words, kp) for kp in range(2)]
        w3_raw = [load_w3(0)]
        p1 = load_list("p1", pos1)
        p2 = load_list("p2", pos2)
        p3 = load_list("p3", pos3)

        v2 = gather_words("v2", v2_raw, idx2)
        v2_scale = gather_scales("v2_scale", v2_plane, idx2)
        w2_scale = deal("w2_scale", w2_plane, U8)
        w2 = deal("w2", w2_raw, U8)
        v_scale = gather_scales("v_scale", v_plane, idx)
        v = [gather_words("v_%d" % kp, v_raw[kp], idx) for kp in range(2)]
        v3_scale = gather_scales("v3_scale", v3_plane, idx3)

        w1_q = {}
        for kp in range(2):
            w1_q[kp, 0] = quantize("w1_%d0" % kp, round_w1(kp, 0))
            w1_raw[kp, 1] = load_w1(kp, 1)
        w3_raw.append(load_w3(1))

        def b_rows(s):
            tile = keep("b%d" % s, [P, S], F32)
            return product_rows(tile, [(
                w2[:, 2 * P * s : 2 * P * (s + 1)].bitcast(FP4X4), w2_scale[:, P * s : P * (s + 1)],
                v2, v2_scale,
            )])

        def a_rows(s):
            half, t = divmod(s, 4)
            cols = slice(P * t, P * (t + 1))
            tile = rows.tile([P, S], F32, name="a_rows")
            return product_rows(tile, [
                (
                    w1_q[kp, half][0][:, cols].bitcast(FP8X4), w1_q[kp, half][1][:, cols],
                    v[kp], v_scale[V_ROW0 + 4 * kp : P, :],
                )
                for kp in range(2)
            ])

        def d_rows(s):
            half, t = divmod(s, 4)
            tile = rows.tile([P, S], F32, name="d_rows")
            return product_rows(tile, [
                (
                    w3[half][:, PASS * kp + P * t : PASS * kp + P * (t + 1)].bitcast(FP8X4),
                    w3_scale[4 * kp : P, P * s : P * (s + 1)], v3[kp], v3_scale[4 * kp : P, :],
                )
                for kp in range(2)
            ])

        b_win = [b_rows(s) for s in range(SLICES)]
        a_win = {s: a_rows(s) for s in range(A_AHEAD)}

        identity = keep("identity", [P, P], F32)
        make_identity(nc, identity[:])
        gain_rows = keep("gain_rows", [P, P], F32)
        nc.gpsimd.memset(gain_rows[:], 0.0)
        for half in range(2):
            nc.gpsimd.dma_start(
                gain_rows[4 * half : 4 * half + 4, :].rearrange("t (g i) -> t g i", i=8),
                gain[PASS * half : PASS * (half + 1)].rearrange("(g t i) -> t g i", t=4, i=8),
            )
        gain_bank = psum.tile([P, P], F32, name="bank")
        nc.tensor.transpose(gain_bank[:], gain_rows[:], identity[:])
        gain_cols = keep("gain_cols", [P, SLICES], F32)
        nc.scalar.copy(gain_cols[:], gain_bank[:, 0:SLICES])

        v3 = [gather_words("v3_%d" % kp, v3_raw[kp], idx3) for kp in range(2)]
        w3_scale = deal("w3_scale", w3_plane, U8)
        w3 = [deal("w3_0", w3_raw[0], U32)]

        w4_raw = [load_w4(half) for half in range(2)]
        base_sb = keep("base_sb", [P, 4, J], F32)
        nc.sync.dma_start(base_sb[:], base.rearrange("(p u) c -> p u c", u=4))

        d_win = {s: d_rows(s) for s in range(D_AHEAD)}

        z_slices = [keep("z_planes%d" % half, [P, 4, J], BF16) for half in range(2)]
        a1, lit, dev = {}, {}, {}

        def pick_a(s):
            a1[s] = picked.tile([P, J], F32, name="a1", bufs=2)
            nc.vector.tensor_copy(a1[s][:], a_win[s][:].indirect(p1[:]))

        def join(s):
            lit[s] = picked.tile([P, J], F32, name="lit")
            nc.vector.tensor_tensor(lit[s][:], b_win[s][:].indirect(p2[:]), a1[s][:], ADD)
            dev[s] = picked.tile([P, J], F32, name="dev")
            nc.vector.tensor_tensor(dev[s][:], d_win[s][:].indirect(p3[:]), a1[s][:], SUBTRACT)

        def take_tanh(s):
            nc.scalar.activation(lit[s][:], lit[s][:], TANH)
            nc.scalar.activation(dev[s][:], dev[s][:], TANH, scale=-1.0)

        def multiply(s):
            nc.vector.scalar_tensor_tensor(
                z_slices[s // 4][:, s % 4, :], lit[s][:], gain_cols[:, s : s + 1], dev[s][:], MULT, MULT
            )

        def weave(engine_copy, four_slices):
            width = four_slices.shape[2]
            out = rounded.tile([P, 4 * width], BF16, name="rounded", align_bytes=64)
            engine_copy(out[:].rearrange("p (c t) -> p c t", t=4), four_slices.rearrange("p t c -> p c t"))
            return out

        y_codes = keep("y_codes", [P, J], U32)
        y_scales = keep("y_scales", [P, J], U8)
        w4_q = {}

        def last_pass(out, u, half, z_q, start, stop):
            nc.tensor.matmul_mx(
                out=out,
                lhsT=w4_q[half][0][:, P * u : P * (u + 1)].bitcast(FP8X4),
                lhsT_scale=w4_q[half][1][:, P * u : P * (u + 1)],
                rhs=z_q[0][:].bitcast(FP8X4), rhs_scale=z_q[1][:],
                start=start, stop=stop,
            )

        pick_a(0)
        for s in range(SLICES):
            join(s)
            if s == 0:
                w3.append(deal("w3_1", w3_raw[1], U32))
            if s < 2:
                w1_q[s, 1] = quantize("w1_%d1" % s, round_w1(s, 1))
            if s + A_AHEAD < SLICES:
                a_win[s + A_AHEAD] = a_rows(s + A_AHEAD)
            if s + D_AHEAD < SLICES:
                d_win[s + D_AHEAD] = d_rows(s + D_AHEAD)
            take_tanh(s)
            if s + 1 < SLICES:
                pick_a(s + 1)
            if s >= 1:
                multiply(s - 1)
            if s in (W4_AT, W4_AT + 1):
                w4_q[s - W4_AT] = quantize("w4_%d" % (s - W4_AT), round_w4(s - W4_AT))
            if s == Z0_AT:
                z0_q = quantize("z0", weave(nc.vector.tensor_copy, z_slices[0][:]))
        multiply(SLICES - 1)

        parts = [slice(c0, c0 + J // 2) for c0 in (0, J // 2)]
        copies = (nc.vector.tensor_copy, nc.scalar.copy)
        y_banks = [psum.tile([P, J], F32, name="bank") for u in range(4)]
        for u in range(4):
            last_pass(y_banks[u][:], u, 0, z0_q, True, False)
        z_woven = [weave(engine_copy, z_slices[1][:, :, cols]) for engine_copy, cols in zip(copies, parts)]
        for n_part, cols in enumerate(parts):
            z1_q = quantize("z1_%d" % n_part, z_woven[n_part])
            for u in range(4):
                last_pass(y_banks[u][:, cols], u, 1, z1_q, False, n_part == len(parts) - 1)
        y = keep("y", [P, 4, J], F32)
        y_out = out_0.rearrange("(p u) c -> p u c", u=4)
        for u in range(4):
            nc.vector.tensor_tensor(y[:, u, :], y_banks[u][:], base_sb[:, u, :], ADD)
            if u % 2 == 1:
                nc.sync.dma_start(y_out[:, u - 1 : u + 1, :], y[:, u - 1 : u + 1, :])
        y_woven = [weave(engine_copy, y[:, :, cols]) for engine_copy, cols in zip(copies, parts)]
        for woven, cols in zip(y_woven, parts):
            nc.vector.quantize_mx(out=y_codes[:, cols].bitcast(FP8X4), scales=y_scales[:, cols], in_=woven[:])
        nc.sync.dma_start(out_1[0].rearrange("p c t -> p (c t)").bitcast(I32), y_codes[:].bitcast(I32))
        for q in range(4):
            queue = nc.sync if q % 2 == 0 else nc.scalar
            queue.dma_start(
                out_2[0, 4 * q : 4 * q + 4, :].bitcast(I32), y_scales[32 * q : 32 * q + 4, :].bitcast(I32)
            )
